import numpy as np
import ml_dtypes


def mxq(x, axis, fmt="e4m3"):
    dtype, down = {"e4m3": (ml_dtypes.float8_e4m3fn, 7), "e5m2": (ml_dtypes.float8_e5m2, 14)}[fmt]
    v = np.moveaxis(np.asarray(x, np.float32).astype(ml_dtypes.bfloat16).astype(np.float64), axis, -1)
    blocks = v.reshape(v.shape[:-1] + (-1, 32))
    amax = np.abs(blocks).max(-1, keepdims=True)
    byte = np.maximum(np.where(amax > 0, np.frexp(amax)[1] - 1 + 127, 0) - down, 1)
    scale = np.exp2(byte - 127.0)
    codes = (blocks / scale).astype(np.float32).astype(dtype).astype(np.float64)
    return np.moveaxis((codes * scale).reshape(v.shape), -1, axis)


WIDE = False


def mx_kscale(k):
    if not WIDE:
        return np.ones(k)
    levels = np.array([10, -10, 5, -5, 0])
    if k % 512:
        return np.exp2(np.random.permutation(np.resize(levels, k // 32))).repeat(32)
    a = np.empty((k // 512, 16))
    for p in range(k // 512):
        a[p, :8] = np.random.permutation(np.resize(levels, 8))
        for g in range(8):
            far = levels[np.abs(levels - a[p, g]) >= 10]
            a[p, g + 8] = far[np.random.randint(len(far))]
    return np.exp2(a.ravel()).repeat(32)


def f64(x):
    return np.asarray(x).astype(np.float64)


def striped(idx):
    return np.tile(idx.reshape(-1, 16).T, (8, 1)).astype(np.uint16)


def unstriped(offs):
    return offs[:16].T.reshape(-1).astype(np.int64)


def pack_weight(w):
    k, n = w.shape
    w = f64(np.asarray(w, np.float32).astype(ml_dtypes.bfloat16)).reshape(k // 32, 32, n)
    amax = np.abs(w).max(1)
    byte = np.clip(np.where(amax > 0, np.frexp(amax)[1] - 1 + 127 - 7, 1), 1, 254)
    scaled = (w * np.exp2(127.0 - byte)[:, None, :]).reshape(k, n).astype(np.float32)
    words = np.ascontiguousarray(scaled.reshape(k // 512, 128, 4, n).transpose(0, 1, 3, 2)).astype(ml_dtypes.float8_e4m3fn).view(np.uint8)
    return words, np.ascontiguousarray(byte.astype(np.uint8).reshape(k // 512, 16, n))


def unpack_weight(words, scales):
    g, p, n, _ = words.shape
    vals = np.ascontiguousarray(words).view(ml_dtypes.float8_e4m3fn).astype(np.float64) * np.repeat(np.exp2(scales.astype(np.float64) - 127.0), 8, axis=1)[..., None]
    return vals.transpose(0, 1, 3, 2).reshape(g * 512, n)


K, T, S, N = 512, 2048, 1024, 128


def setup_inputs():
    n = np.random.standard_normal
    s = mx_kscale(K)[:, None]
    packed_xT = pack_weight(n((K, T)) * s)
    return {
        "x_words": packed_xT[0],
        "x_scales": packed_xT[1],
        "w1": (n((K, N)) / np.sqrt(K) / s).astype(np.float32),
        "w2": (n((K, N)) / np.sqrt(K) / s).astype(np.float32),
        "tap0": (0.4 * n((N, 1))).astype(np.float32),
        "tap1": (0.4 * n((N, 1))).astype(np.float32),
        "tap2": (0.4 * n((N, 1))).astype(np.float32),
        "tap3": (0.4 * n((N, 1))).astype(np.float32),
        "offs": striped(np.random.permutation(T)[:S]),
    }


def reference(x_words, x_scales, w1, w2, tap0, tap1, tap2, tap3, offs):
    xq = unpack_weight(x_words, x_scales)[:, unstriped(offs)]
    mic = mxq(f64(w2), 0, "e4m3").T @ xq
    far = mxq(f64(w1), 0, "e4m3").T @ xq
    echo = f64(tap0) * far + f64(tap1) * (np.pad(far, ((0, 0), (1, 0)))[:, :S]) + f64(tap2) * (np.pad(far, ((0, 0), (2, 0)))[:, :S]) + f64(tap3) * (np.pad(far, ((0, 0), (3, 0)))[:, :S])
    err = mic - echo
    pw = (far) ** 2 + (np.pad(far, ((0, 0), (1, 0)))[:, :S]) ** 2 + (np.pad(far, ((0, 0), (2, 0)))[:, :S]) ** 2 + (np.pad(far, ((0, 0), (3, 0)))[:, :S]) ** 2 + 0.5
    st = err / pw
    return err - (0.6 * (st * (pw - 0.5)))

@@ -1,0 +1,187 @@
+from contextlib import ExitStack
+
+import concourse.mybir as mybir
+
+K, T, S, N = 512, 2048, 1024, 128
+FLOPS = 2 * 2 * K * N * S
+
+F32 = mybir.dt.float32
+BF16 = mybir.dt.bfloat16
+I32 = mybir.dt.int32
+U32 = mybir.dt.uint32
+U16 = mybir.dt.uint16
+U8 = mybir.dt.uint8
+FP8X4 = mybir.dt.float8_e4m3fn_x4
+ACT = mybir.ActivationFunctionType
+ALU = mybir.AluOpType
+
+P = 128
+PACK = 4
+PAD = 8
+CHUNK = 256
+CHUNKS = S // CHUNK
+HALF = S // 2
+
+
+def tile_picked_ynlms_post_p_kernel(
+    tc, x_words, x_scales, w1, w2, tap0, tap1, tap2, tap3, offs, out
+):
+    nc = tc.nc
+    with ExitStack() as ctx:
+        keep = ctx.enter_context(tc.tile_pool(name="keep", bufs=1))
+        psum = ctx.enter_context(tc.psum_pool(name="psum", bufs=1))
+
+        offsets = keep.tile([P, S // 16], U16, name="offsets")
+        nc.sync.dma_start(offsets[:], offs)
+
+        scale_table = keep.tile([P, T], U8, name="scale_table", align_bytes=64)
+        nc.vector.memset(scale_table[:].bitcast(I32), 0)
+        for q in range(4):
+            nc.sync.dma_start(
+                scale_table[32 * q : 32 * q + 4, :].bitcast(I32),
+                x_scales[0, 4 * q : 4 * q + 4, :].bitcast(I32),
+            )
+
+        w_raw = []
+        for i, w in enumerate((w1, w2)):
+            raw = keep.tile([P, PACK, N], F32, name="w_raw%d" % i)
+            nc.sync.dma_start(raw[:], w.rearrange("(p j) n -> p j n", j=PACK))
+            w_raw.append(raw)
+
+        neg_far = keep.tile([P, PAD + S], F32, name="neg_far")
+        square = keep.tile([P, PAD + S], F32, name="square")
+        pair = keep.tile([P, PAD + S], F32, name="pair")
+        zeros = keep.tile([P, PAD], F32, name="zeros", tag="words", align_bytes=64)
+        nc.vector.memset(zeros[:], 0.0)
+        for padded in (neg_far, square, pair):
+            nc.vector.tensor_copy(padded[:, :PAD], zeros[:])
+        warm = keep.tile([P, 1], F32, name="warm")
+        nc.scalar.activation(warm[:], neg_far[:, :1], ACT.Abs_reciprocal_sqrt, bias=1.0)
+
+        word_table = keep.tile([P, T], I32, name="word_table", tag="words", align_bytes=64)
+        nc.sync.dma_start(
+            word_table[:], x_words[0].rearrange("p n t -> p (n t)").bitcast(I32)
+        )
+
+        taps = []
+        for d, tap in enumerate((tap0, tap1, tap2, tap3)):
+            column = keep.tile([P, 1], F32, name="tap%d" % d)
+            nc.gpsimd.dma_start(column[:], tap)
+            taps.append(column)
+
+        x_bytes = keep.tile([P, S], U8, name="x_bytes", align_bytes=64)
+        nc.vector.tensor_copy(x_bytes[:], scale_table[:].indirect(offsets[:]))
+
+        w_codes, w_bytes = [], []
+        for i in range(2):
+            grouped = keep.tile([P, N, PACK], BF16, name="grouped%d" % i, align_bytes=64)
+            nc.scalar.copy(grouped[:], w_raw[i][:].rearrange("p j n -> p n j"))
+            codes = keep.tile([P, N], U32, name="w_codes%d" % i, align_bytes=64)
+            plane = keep.tile([P, N], U8, name="w_bytes%d" % i, align_bytes=64)
+            nc.vector.quantize_mx(
+                out=codes[:].bitcast(FP8X4),
+                scales=plane[:],
+                in_=grouped[:].rearrange("p n j -> p (n j)"),
+            )
+            w_codes.append(codes)
+            w_bytes.append(plane)
+
+        x_codes = keep.tile([P, S], U32, name="x_codes", align_bytes=64)
+        mic = []
+        for c in range(CHUNKS):
+            cols = slice(c * CHUNK, (c + 1) * CHUNK)
+            nc.vector.tensor_copy(
+                x_codes[:, cols],
+                word_table[:].bitcast(U32).indirect(
+                    offsets[:, c * CHUNK // 16 : (c + 1) * CHUNK // 16]
+                ),
+            )
+            banks = []
+            for i in range(2):
+                bank = psum.tile([P, CHUNK], F32, name="bank%d_%d" % (i, c))
+                nc.tensor.matmul_mx(
+                    out=bank[:],
+                    lhsT=w_codes[i][:].bitcast(FP8X4),
+                    lhsT_scale=w_bytes[i][:],
+                    rhs=x_codes[:, cols].bitcast(FP8X4),
+                    rhs_scale=x_bytes[:, cols],
+                    start=True,
+                    stop=True,
+                )
+                banks.append(bank)
+            here = slice(PAD + c * CHUNK, PAD + (c + 1) * CHUNK)
+            nc.scalar.activation(square[:, here], banks[0][:], ACT.Square)
+            nc.scalar.activation(neg_far[:, here], banks[0][:], ACT.Copy, scale=-1.0)
+            mic.append(banks[1])
+
+        energy = keep.tile([P, S], F32, name="energy")
+        root = keep.tile([P, S], F32, name="root")
+        gain = keep.tile([P, S], F32, name="gain")
+        err = [keep.tile([P, S], F32, name="err%d" % i) for i in range(2)]
+        result = keep.tile([P, S], F32, name="result")
+
+        def back(tile, start, width, delay):
+            return tile[:, PAD + start - delay : PAD + start - delay + width]
+
+        def pair_sums(h):
+            nc.vector.tensor_tensor(
+                back(pair, h * HALF, HALF, 0),
+                back(square, h * HALF, HALF, 0),
+                back(square, h * HALF, HALF, 1),
+                ALU.add,
+            )
+
+        def energy_gain(h):
+            cols = slice(h * HALF, (h + 1) * HALF)
+            nc.vector.tensor_tensor(
+                energy[:, cols],
+                back(pair, h * HALF, HALF, 0),
+                back(pair, h * HALF, HALF, 2),
+                ALU.add,
+            )
+            nc.scalar.activation(
+                root[:, cols], energy[:, cols], ACT.Abs_reciprocal_sqrt,
+                scale=1.0 / 0.3, bias=0.5 / 0.3,
+            )
+            nc.scalar.activation(gain[:, cols], root[:, cols], ACT.Square)
+
+        def tap_step(d, c):
+            cols = slice(c * CHUNK, (c + 1) * CHUNK)
+            so_far = mic[c][:] if d == 0 else err[(d - 1) % 2][:, cols]
+            nc.vector.scalar_tensor_tensor(
+                err[d % 2][:, cols],
+                back(neg_far, c * CHUNK, CHUNK, d),
+                taps[d][:],
+                so_far,
+                ALU.mult,
+                ALU.add,
+            )
+
+        def finish(c):
+            cols = slice(c * CHUNK, (c + 1) * CHUNK)
+            nc.vector.scalar_tensor_tensor(
+                result[:, cols], gain[:, cols], 0.4, err[1][:, cols], ALU.add, ALU.mult
+            )
+            nc.sync.dma_start(out[:, cols], result[:, cols])
+
+        pair_sums(0)
+        tap_step(0, 0)
+        energy_gain(0)
+        tap_step(0, 1)
+        tap_step(1, 0)
+        tap_step(1, 1)
+        pair_sums(1)
+        tap_step(2, 0)
+        tap_step(2, 1)
+        energy_gain(1)
+        tap_step(3, 0)
+        tap_step(3, 1)
+        tap_step(0, 2)
+        tap_step(0, 3)
+        finish(0)
+        finish(1)
+        for d in range(1, 4):
+            tap_step(d, 2)
+            tap_step(d, 3)
+        finish(2)
+        finish(3)

@@ -1,6 +1,7 @@
 from contextlib import ExitStack
 
 import concourse.mybir as mybir
+from concourse.masks import make_identity
 
 K, T, S, N = 512, 2048, 1024, 128
 FLOPS = 2 * 2 * K * N * S
@@ -20,7 +21,7 @@ PACK = 4
 PAD = 8
 CHUNK = 256
 CHUNKS = S // CHUNK
-HALF = S // 2
+BLOCKS = CHUNK // P
 
 
 def tile_picked_ynlms_post_p_kernel(
@@ -42,146 +43,178 @@ def tile_picked_ynlms_post_p_kernel(
                 x_scales[0, 4 * q : 4 * q + 4, :].bitcast(I32),
             )
 
-        w_raw = []
-        for i, w in enumerate((w1, w2)):
-            raw = keep.tile([P, PACK, N], F32, name="w_raw%d" % i)
-            nc.sync.dma_start(raw[:], w.rearrange("(p j) n -> p j n", j=PACK))
-            w_raw.append(raw)
+        identity = keep.tile([P, P], F32, name="identity")
+        make_identity(nc, identity[:])
+        taps = [keep.tile([P, 1], F32, name="tap%d" % d) for d in range(4)]
+        nc.gpsimd.dma_start(taps[3][:], tap3)
+        nc.gpsimd.dma_start(taps[2][:], tap2)
+        nc.gpsimd.dma_start(taps[1][:], tap1)
+        nc.gpsimd.dma_start(taps[0][:], tap0)
 
-        neg_far = keep.tile([P, PAD + S], F32, name="neg_far")
-        square = keep.tile([P, PAD + S], F32, name="square")
-        pair = keep.tile([P, PAD + S], F32, name="pair")
-        zeros = keep.tile([P, PAD], F32, name="zeros", tag="words", align_bytes=64)
+        streams = keep.tile([P, 5, PAD + S], F32, name="streams")
+        zeros = keep.tile([P, 5, PAD], F32, name="zeros", tag="words")
         nc.vector.memset(zeros[:], 0.0)
-        for padded in (neg_far, square, pair):
-            nc.vector.tensor_copy(padded[:, :PAD], zeros[:])
+        nc.vector.tensor_copy(streams[:, :, :PAD], zeros[:])
         warm = keep.tile([P, 1], F32, name="warm")
-        nc.scalar.activation(warm[:], neg_far[:, :1], ACT.Abs_reciprocal_sqrt, bias=1.0)
+        nc.scalar.activation(warm[:], streams[:, 0, :1], ACT.Abs_reciprocal_sqrt, bias=1.0)
 
-        word_table = keep.tile([P, T], I32, name="word_table", tag="words", align_bytes=64)
-        nc.sync.dma_start(
-            word_table[:], x_words[0].rearrange("p n t -> p (n t)").bitcast(I32)
-        )
+        def frames(row, start, width, delay=0):
+            return streams[:, row, PAD + start - delay : PAD + start - delay + width]
 
-        taps = []
-        for d, tap in enumerate((tap0, tap1, tap2, tap3)):
-            column = keep.tile([P, 1], F32, name="tap%d" % d)
-            nc.gpsimd.dma_start(column[:], tap)
-            taps.append(column)
+        SQUARE, PAIR = 0, 4
 
-        x_bytes = keep.tile([P, S], U8, name="x_bytes", align_bytes=64)
-        nc.vector.tensor_copy(x_bytes[:], scale_table[:].indirect(offsets[:]))
+        def load_weights(w, raw, name):
+            nc.sync.dma_start(raw[:], w.rearrange("(p j) n -> p j n", j=PACK))
+            grouped = keep.tile([P, N, PACK], BF16, name=name + "_grouped", align_bytes=64)
+            nc.scalar.copy(grouped[:], raw[:].rearrange("p j n -> p n j"))
+            return grouped
 
-        w_codes, w_bytes = [], []
-        for i in range(2):
-            grouped = keep.tile([P, N, PACK], BF16, name="grouped%d" % i, align_bytes=64)
-            nc.scalar.copy(grouped[:], w_raw[i][:].rearrange("p j n -> p n j"))
-            codes = keep.tile([P, N], U32, name="w_codes%d" % i, align_bytes=64)
-            plane = keep.tile([P, N], U8, name="w_bytes%d" % i, align_bytes=64)
+        def quantize(grouped, name):
+            codes = keep.tile([P, N], U32, name=name + "_codes", align_bytes=64)
+            plane = keep.tile([P, N], U8, name=name + "_bytes", align_bytes=64)
             nc.vector.quantize_mx(
                 out=codes[:].bitcast(FP8X4),
                 scales=plane[:],
                 in_=grouped[:].rearrange("p n j -> p (n j)"),
             )
-            w_codes.append(codes)
-            w_bytes.append(plane)
+            return codes, plane
+
+        w1_raw = keep.tile([P, PACK, N], F32, name="w1_raw")
+        w1_grouped = load_weights(w1, w1_raw, "w1")
+        w2_raw = keep.tile([P, PACK, N], F32, name="w2_raw")
+        w2_grouped = load_weights(w2, w2_raw, "w2")
+        word_table = keep.tile([P, T], I32, name="word_table", tag="words")
+        nc.sync.dma_start(
+            word_table[:], x_words[0].rearrange("p n t -> p (n t)").bitcast(I32)
+        )
+
+        x_bytes = keep.tile([P, S], U8, name="x_bytes", align_bytes=64)
+        nc.vector.tensor_copy(x_bytes[:], scale_table[:].indirect(offsets[:]))
+        w1_mx = quantize(w1_grouped, "w1")
+        w2_mx = quantize(w2_grouped, "w2")
 
         x_codes = keep.tile([P, S], U32, name="x_codes", align_bytes=64)
-        mic = []
-        for c in range(CHUNKS):
+
+        def product(bank, weights, c):
             cols = slice(c * CHUNK, (c + 1) * CHUNK)
+            nc.tensor.matmul_mx(
+                out=bank,
+                lhsT=weights[0][:].bitcast(FP8X4),
+                lhsT_scale=weights[1][:],
+                rhs=x_codes[:, cols].bitcast(FP8X4),
+                rhs_scale=x_bytes[:, cols],
+                start=True,
+                stop=True,
+            )
+
+        far = []
+        mic_banks = [psum.tile([P, 2 * CHUNK], F32, name="mic%d" % h) for h in range(2)]
+        mic = [mic_banks[c // 2][:, (c % 2) * CHUNK : (c % 2 + 1) * CHUNK] for c in range(CHUNKS)]
+        for c in range(CHUNKS):
             nc.vector.tensor_copy(
-                x_codes[:, cols],
+                x_codes[:, c * CHUNK : (c + 1) * CHUNK],
                 word_table[:].bitcast(U32).indirect(
                     offsets[:, c * CHUNK // 16 : (c + 1) * CHUNK // 16]
                 ),
             )
-            banks = []
-            for i in range(2):
-                bank = psum.tile([P, CHUNK], F32, name="bank%d_%d" % (i, c))
-                nc.tensor.matmul_mx(
-                    out=bank[:],
-                    lhsT=w_codes[i][:].bitcast(FP8X4),
-                    lhsT_scale=w_bytes[i][:],
-                    rhs=x_codes[:, cols].bitcast(FP8X4),
-                    rhs_scale=x_bytes[:, cols],
-                    start=True,
-                    stop=True,
-                )
-                banks.append(bank)
-            here = slice(PAD + c * CHUNK, PAD + (c + 1) * CHUNK)
-            nc.scalar.activation(square[:, here], banks[0][:], ACT.Square)
-            nc.scalar.activation(neg_far[:, here], banks[0][:], ACT.Copy, scale=-1.0)
-            mic.append(banks[1])
+            bank = psum.tile([P, CHUNK], F32, name="far%d" % c)
+            product(bank[:], w1_mx, c)
+            product(mic[c], w2_mx, c)
+            nc.scalar.activation(frames(SQUARE, c * CHUNK, CHUNK), bank[:], ACT.Square)
+            nc.scalar.activation(frames(3, c * CHUNK, CHUNK), bank[:], ACT.Copy, scale=taps[3][:])
+            far.append(bank)
 
         energy = keep.tile([P, S], F32, name="energy")
-        root = keep.tile([P, S], F32, name="root")
+        root_sb = keep.tile([P, S], F32, name="root_sb")
         gain = keep.tile([P, S], F32, name="gain")
-        err = [keep.tile([P, S], F32, name="err%d" % i) for i in range(2)]
-        result = keep.tile([P, S], F32, name="result")
 
-        def back(tile, start, width, delay):
-            return tile[:, PAD + start - delay : PAD + start - delay + width]
-
-        def pair_sums(h):
-            nc.vector.tensor_tensor(
-                back(pair, h * HALF, HALF, 0),
-                back(square, h * HALF, HALF, 0),
-                back(square, h * HALF, HALF, 1),
-                ALU.add,
-            )
-
-        def energy_gain(h):
-            cols = slice(h * HALF, (h + 1) * HALF)
-            nc.vector.tensor_tensor(
-                energy[:, cols],
-                back(pair, h * HALF, HALF, 0),
-                back(pair, h * HALF, HALF, 2),
-                ALU.add,
-            )
+        def inverse_root(cols, source):
             nc.scalar.activation(
-                root[:, cols], energy[:, cols], ACT.Abs_reciprocal_sqrt,
+                root_sb[:, cols], source, ACT.Abs_reciprocal_sqrt,
                 scale=1.0 / 0.3, bias=0.5 / 0.3,
             )
-            nc.scalar.activation(gain[:, cols], root[:, cols], ACT.Square)
+
+        def gain_on_gpsimd(c):
+            lo, hi = c * CHUNK, (c + 1) * CHUNK
+            first = lo - 2 if c == 2 else lo
+            nc.gpsimd.tensor_tensor(
+                frames(PAIR, first, hi - first),
+                frames(SQUARE, first, hi - first),
+                frames(SQUARE, first, hi - first, 1),
+                ALU.add,
+            )
+            nc.gpsimd.tensor_tensor(
+                energy[:, lo:hi], frames(PAIR, lo, CHUNK), frames(PAIR, lo, CHUNK, 2), ALU.add
+            )
+            inverse_root(slice(lo, hi), energy[:, lo:hi])
+            nc.scalar.activation(gain[:, lo:hi], root_sb[:, lo:hi], ACT.Square)
+
+        gain_on_gpsimd(0)
+        energy_t = psum.tile([P, CHUNK], F32, name="energy_t")
+        for b in range(BLOCKS):
+            for delay in range(4):
+                nc.tensor.matmul(
+                    energy_t[:, b * P : (b + 1) * P],
+                    frames(SQUARE, CHUNK + b * P, P, delay),
+                    identity[:],
+                    start=(delay == 0),
+                    stop=(delay == 3),
+                    is_transpose=True,
+                )
+        inverse_root(slice(CHUNK, 2 * CHUNK), energy_t[:])
+        root = psum.tile([P, CHUNK], F32, name="root")
+        for b in range(BLOCKS):
+            nc.tensor.transpose(
+                root[:, b * P : (b + 1) * P], root_sb[:, CHUNK + b * P : CHUNK + (b + 1) * P], identity[:]
+            )
+        nc.scalar.activation(gain[:, CHUNK : 2 * CHUNK], root[:], ACT.Square)
+
+        gain_on_gpsimd(2)
+        gain_on_gpsimd(3)
+
+        echo = keep.tile([P, S], F32, name="echo")
+        err = keep.tile([P, S], F32, name="err")
+        result = keep.tile([P, S], F32, name="result")
 
         def tap_step(d, c):
             cols = slice(c * CHUNK, (c + 1) * CHUNK)
-            so_far = mic[c][:] if d == 0 else err[(d - 1) % 2][:, cols]
             nc.vector.scalar_tensor_tensor(
-                err[d % 2][:, cols],
-                back(neg_far, c * CHUNK, CHUNK, d),
+                frames(d, c * CHUNK, CHUNK) if d else echo[:, cols],
+                far[c][:],
                 taps[d][:],
-                so_far,
+                frames(d + 1, c * CHUNK, CHUNK, 1),
                 ALU.mult,
                 ALU.add,
             )
 
+        def error(c):
+            cols = slice(c * CHUNK, (c + 1) * CHUNK)
+            nc.vector.tensor_tensor(err[:, cols], mic[c], echo[:, cols], ALU.subtract)
+
         def finish(c):
             cols = slice(c * CHUNK, (c + 1) * CHUNK)
             nc.vector.scalar_tensor_tensor(
-                result[:, cols], gain[:, cols], 0.4, err[1][:, cols], ALU.add, ALU.mult
+                result[:, cols], gain[:, cols], 0.4, err[:, cols], ALU.add, ALU.mult
             )
             nc.sync.dma_start(out[:, cols], result[:, cols])
 
-        pair_sums(0)
-        tap_step(0, 0)
-        energy_gain(0)
-        tap_step(0, 1)
-        tap_step(1, 0)
-        tap_step(1, 1)
-        pair_sums(1)
         tap_step(2, 0)
+        tap_step(1, 0)
         tap_step(2, 1)
-        energy_gain(1)
-        tap_step(3, 0)
-        tap_step(3, 1)
+        tap_step(0, 0)
+        tap_step(1, 1)
+        error(0)
+        tap_step(0, 1)
+        tap_step(2, 2)
+        error(1)
+        tap_step(1, 2)
+        tap_step(2, 3)
         tap_step(0, 2)
+        tap_step(1, 3)
+        error(2)
         tap_step(0, 3)
         finish(0)
+        error(3)
         finish(1)
-        for d in range(1, 4):
-            tap_step(d, 2)
-            tap_step(d, 3)
         finish(2)
         finish(3)

@@ -18,10 +18,11 @@ ALU = mybir.AluOpType
 
 P = 128
 PACK = 4
-PAD = 8
+PAD = 16
 CHUNK = 256
 CHUNKS = S // CHUNK
 BLOCKS = CHUNK // P
+RAW_BYTES = PACK * N * 4
 
 
 def tile_picked_ynlms_post_p_kernel(
@@ -30,6 +31,7 @@ def tile_picked_ynlms_post_p_kernel(
     nc = tc.nc
     with ExitStack() as ctx:
         keep = ctx.enter_context(tc.tile_pool(name="keep", bufs=1))
+        late = ctx.enter_context(tc.tile_pool(name="late", bufs=1))
         psum = ctx.enter_context(tc.psum_pool(name="psum", bufs=1))
 
         offsets = keep.tile([P, S // 16], U16, name="offsets")
@@ -37,22 +39,16 @@ def tile_picked_ynlms_post_p_kernel(
 
         scale_table = keep.tile([P, T], U8, name="scale_table", align_bytes=64)
         nc.vector.memset(scale_table[:].bitcast(I32), 0)
-        for q in range(4):
+        for r in range(4):
             nc.sync.dma_start(
-                scale_table[32 * q : 32 * q + 4, :].bitcast(I32),
-                x_scales[0, 4 * q : 4 * q + 4, :].bitcast(I32),
+                scale_table[r:P:32, :].bitcast(I32), x_scales[0, r:16:4, :].bitcast(I32)
             )
 
         identity = keep.tile([P, P], F32, name="identity")
         make_identity(nc, identity[:])
-        taps = [keep.tile([P, 1], F32, name="tap%d" % d) for d in range(4)]
-        nc.gpsimd.dma_start(taps[3][:], tap3)
-        nc.gpsimd.dma_start(taps[2][:], tap2)
-        nc.gpsimd.dma_start(taps[1][:], tap1)
-        nc.gpsimd.dma_start(taps[0][:], tap0)
 
         streams = keep.tile([P, 5, PAD + S], F32, name="streams")
-        zeros = keep.tile([P, 5, PAD], F32, name="zeros", tag="words")
+        zeros = late.tile([P, 5, PAD], F32, name="zeros", offset=RAW_BYTES - 32)
         nc.vector.memset(zeros[:], 0.0)
         nc.vector.tensor_copy(streams[:, :, :PAD], zeros[:])
         warm = keep.tile([P, 1], F32, name="warm")
@@ -65,33 +61,34 @@ def tile_picked_ynlms_post_p_kernel(
 
         def load_weights(w, raw, name):
             nc.sync.dma_start(raw[:], w.rearrange("(p j) n -> p j n", j=PACK))
-            grouped = keep.tile([P, N, PACK], BF16, name=name + "_grouped", align_bytes=64)
-            nc.scalar.copy(grouped[:], raw[:].rearrange("p j n -> p n j"))
-            return grouped
+            nc.scalar.copy(name, raw[:].rearrange("p j n -> p n j"))
 
-        def quantize(grouped, name):
-            codes = keep.tile([P, N], U32, name=name + "_codes", align_bytes=64)
-            plane = keep.tile([P, N], U8, name=name + "_bytes", align_bytes=64)
-            nc.vector.quantize_mx(
-                out=codes[:].bitcast(FP8X4),
-                scales=plane[:],
-                in_=grouped[:].rearrange("p n j -> p (n j)"),
-            )
-            return codes, plane
-
+        grouped = keep.tile([P, 2 * N, PACK], BF16, name="grouped", align_bytes=64)
         w1_raw = keep.tile([P, PACK, N], F32, name="w1_raw")
-        w1_grouped = load_weights(w1, w1_raw, "w1")
-        w2_raw = keep.tile([P, PACK, N], F32, name="w2_raw")
-        w2_grouped = load_weights(w2, w2_raw, "w2")
-        word_table = keep.tile([P, T], I32, name="word_table", tag="words")
+        load_weights(w1, w1_raw, grouped[:, :N, :])
+        w2_raw = late.tile([P, PACK, N], F32, name="w2_raw", offset=0)
+        load_weights(w2, w2_raw, grouped[:, N:, :])
+        word_table = late.tile([P, T], I32, name="word_table", offset=RAW_BYTES + 4 * 32)
         nc.sync.dma_start(
             word_table[:], x_words[0].rearrange("p n t -> p (n t)").bitcast(I32)
         )
+        taps = [
+            late.tile([P, 1], F32, name="tap%d" % d, offset=RAW_BYTES + 32 * d) for d in range(4)
+        ]
+        for d, tap in ((3, tap3), (2, tap2), (1, tap1), (0, tap0)):
+            nc.sync.dma_start(taps[d][:], tap)
 
         x_bytes = keep.tile([P, S], U8, name="x_bytes", align_bytes=64)
         nc.vector.tensor_copy(x_bytes[:], scale_table[:].indirect(offsets[:]))
-        w1_mx = quantize(w1_grouped, "w1")
-        w2_mx = quantize(w2_grouped, "w2")
+        w_codes = keep.tile([P, 2 * N], U32, name="w_codes", align_bytes=64)
+        w_bytes = keep.tile([P, 2 * N], U8, name="w_bytes", align_bytes=64)
+        nc.vector.quantize_mx(
+            out=w_codes[:].bitcast(FP8X4),
+            scales=w_bytes[:],
+            in_=grouped[:].rearrange("p n j -> p (n j)"),
+        )
+        w1_mx = (w_codes[:, :N], w_bytes[:, :N])
+        w2_mx = (w_codes[:, N:], w_bytes[:, N:])
 
         x_codes = keep.tile([P, S], U32, name="x_codes", align_bytes=64)
 
@@ -99,8 +96,8 @@ def tile_picked_ynlms_post_p_kernel(
             cols = slice(c * CHUNK, (c + 1) * CHUNK)
             nc.tensor.matmul_mx(
                 out=bank,
-                lhsT=weights[0][:].bitcast(FP8X4),
-                lhsT_scale=weights[1][:],
+                lhsT=weights[0].bitcast(FP8X4),
+                lhsT_scale=weights[1],
                 rhs=x_codes[:, cols].bitcast(FP8X4),
                 rhs_scale=x_bytes[:, cols],
                 start=True,
@@ -149,28 +146,33 @@ def tile_picked_ynlms_post_p_kernel(
             inverse_root(slice(lo, hi), energy[:, lo:hi])
             nc.scalar.activation(gain[:, lo:hi], root_sb[:, lo:hi], ACT.Square)
 
-        gain_on_gpsimd(0)
-        energy_t = psum.tile([P, CHUNK], F32, name="energy_t")
-        for b in range(BLOCKS):
-            for delay in range(4):
-                nc.tensor.matmul(
-                    energy_t[:, b * P : (b + 1) * P],
-                    frames(SQUARE, CHUNK + b * P, P, delay),
+        def gain_by_transposes(c):
+            lo, hi = c * CHUNK, (c + 1) * CHUNK
+            energy_t = psum.tile([P, CHUNK], F32, name="energy_t", tag="turned%d" % c)
+            for b in range(BLOCKS):
+                for delay in range(4):
+                    nc.tensor.matmul(
+                        energy_t[:, b * P : (b + 1) * P],
+                        frames(SQUARE, lo + b * P, P, delay),
+                        identity[:],
+                        start=(delay == 0),
+                        stop=(delay == 3),
+                        is_transpose=True,
+                    )
+            inverse_root(slice(lo, hi), energy_t[:])
+            root = psum.tile([P, CHUNK], F32, name="root", tag="turned%d" % c)
+            for b in range(BLOCKS):
+                nc.tensor.transpose(
+                    root[:, b * P : (b + 1) * P],
+                    root_sb[:, lo + b * P : lo + (b + 1) * P],
                     identity[:],
-                    start=(delay == 0),
-                    stop=(delay == 3),
-                    is_transpose=True,
                 )
-        inverse_root(slice(CHUNK, 2 * CHUNK), energy_t[:])
-        root = psum.tile([P, CHUNK], F32, name="root")
-        for b in range(BLOCKS):
-            nc.tensor.transpose(
-                root[:, b * P : (b + 1) * P], root_sb[:, CHUNK + b * P : CHUNK + (b + 1) * P], identity[:]
-            )
-        nc.scalar.activation(gain[:, CHUNK : 2 * CHUNK], root[:], ACT.Square)
+            nc.scalar.activation(gain[:, lo:hi], root[:], ACT.Square)
 
+        gain_on_gpsimd(0)
+        gain_by_transposes(1)
+        gain_by_transposes(3)
         gain_on_gpsimd(2)
-        gain_on_gpsimd(3)
 
         echo = keep.tile([P, S], F32, name="echo")
         err = keep.tile([P, S], F32, name="err")
@@ -216,5 +218,5 @@ def tile_picked_ynlms_post_p_kernel(
         finish(0)
         error(3)
         finish(1)
-        finish(2)
         finish(3)
+        finish(2)

from contextlib import ExitStack

import concourse.mybir as mybir
from concourse.masks import make_identity

K, T, S, N = 512, 2048, 1024, 128
FLOPS = 2 * 2 * K * N * S

F32 = mybir.dt.float32
BF16 = mybir.dt.bfloat16
I32 = mybir.dt.int32
U32 = mybir.dt.uint32
U16 = mybir.dt.uint16
U8 = mybir.dt.uint8
FP8X4 = mybir.dt.float8_e4m3fn_x4
ACT = mybir.ActivationFunctionType
ALU = mybir.AluOpType

P = 128
PACK = 4
PAD = 16
CHUNK = 256
CHUNKS = S // CHUNK
BLOCKS = CHUNK // P
RAW_BYTES = PACK * N * 4


def tile_picked_ynlms_post_p_kernel(
    tc, x_words, x_scales, w1, w2, tap0, tap1, tap2, tap3, offs, out
):
    nc = tc.nc
    with ExitStack() as ctx:
        keep = ctx.enter_context(tc.tile_pool(name="keep", bufs=1))
        late = ctx.enter_context(tc.tile_pool(name="late", bufs=1))
        psum = ctx.enter_context(tc.psum_pool(name="psum", bufs=1))

        offsets = keep.tile([P, S // 16], U16, name="offsets")
        nc.sync.dma_start(offsets[:], offs)

        scale_table = keep.tile([P, T], U8, name="scale_table", align_bytes=64)
        nc.vector.memset(scale_table[:].bitcast(I32), 0)
        for r in range(4):
            nc.sync.dma_start(
                scale_table[r:P:32, :].bitcast(I32), x_scales[0, r:16:4, :].bitcast(I32)
            )

        identity = keep.tile([P, P], F32, name="identity")
        make_identity(nc, identity[:])

        streams = keep.tile([P, 5, PAD + S], F32, name="streams")
        zeros = late.tile([P, 5, PAD], F32, name="zeros", offset=RAW_BYTES - 32)
        nc.vector.memset(zeros[:], 0.0)
        nc.vector.tensor_copy(streams[:, :, :PAD], zeros[:])
        warm = keep.tile([P, 1], F32, name="warm")
        nc.scalar.activation(warm[:], streams[:, 0, :1], ACT.Abs_reciprocal_sqrt, bias=1.0)

        def frames(row, start, width, delay=0):
            return streams[:, row, PAD + start - delay : PAD + start - delay + width]

        SQUARE, PAIR = 0, 4

        def load_weights(w, raw, name):
            nc.sync.dma_start(raw[:], w.rearrange("(p j) n -> p j n", j=PACK))
            nc.scalar.copy(name, raw[:].rearrange("p j n -> p n j"))

        grouped = keep.tile([P, 2 * N, PACK], BF16, name="grouped", align_bytes=64)
        w1_raw = keep.tile([P, PACK, N], F32, name="w1_raw")
        load_weights(w1, w1_raw, grouped[:, :N, :])
        w2_raw = late.tile([P, PACK, N], F32, name="w2_raw", offset=0)
        load_weights(w2, w2_raw, grouped[:, N:, :])
        word_table = late.tile([P, T], I32, name="word_table", offset=RAW_BYTES + 4 * 32)
        nc.sync.dma_start(
            word_table[:], x_words[0].rearrange("p n t -> p (n t)").bitcast(I32)
        )
        taps = [
            late.tile([P, 1], F32, name="tap%d" % d, offset=RAW_BYTES + 32 * d) for d in range(4)
        ]
        for d, tap in ((3, tap3), (2, tap2), (1, tap1), (0, tap0)):
            nc.sync.dma_start(taps[d][:], tap)

        x_bytes = keep.tile([P, S], U8, name="x_bytes", align_bytes=64)
        nc.vector.tensor_copy(x_bytes[:], scale_table[:].indirect(offsets[:]))
        w_codes = keep.tile([P, 2 * N], U32, name="w_codes", align_bytes=64)
        w_bytes = keep.tile([P, 2 * N], U8, name="w_bytes", align_bytes=64)
        nc.vector.quantize_mx(
            out=w_codes[:].bitcast(FP8X4),
            scales=w_bytes[:],
            in_=grouped[:].rearrange("p n j -> p (n j)"),
        )
        w1_mx = (w_codes[:, :N], w_bytes[:, :N])
        w2_mx = (w_codes[:, N:], w_bytes[:, N:])

        x_codes = keep.tile([P, S], U32, name="x_codes", align_bytes=64)

        def product(bank, weights, c):
            cols = slice(c * CHUNK, (c + 1) * CHUNK)
            nc.tensor.matmul_mx(
                out=bank,
                lhsT=weights[0].bitcast(FP8X4),
                lhsT_scale=weights[1],
                rhs=x_codes[:, cols].bitcast(FP8X4),
                rhs_scale=x_bytes[:, cols],
                start=True,
                stop=True,
            )

        far = []
        mic_banks = [psum.tile([P, 2 * CHUNK], F32, name="mic%d" % h) for h in range(2)]
        mic = [mic_banks[c // 2][:, (c % 2) * CHUNK : (c % 2 + 1) * CHUNK] for c in range(CHUNKS)]
        for c in range(CHUNKS):
            nc.vector.tensor_copy(
                x_codes[:, c * CHUNK : (c + 1) * CHUNK],
                word_table[:].bitcast(U32).indirect(
                    offsets[:, c * CHUNK // 16 : (c + 1) * CHUNK // 16]
                ),
            )
            bank = psum.tile([P, CHUNK], F32, name="far%d" % c)
            product(bank[:], w1_mx, c)
            product(mic[c], w2_mx, c)
            nc.scalar.activation(frames(SQUARE, c * CHUNK, CHUNK), bank[:], ACT.Square)
            nc.scalar.activation(frames(3, c * CHUNK, CHUNK), bank[:], ACT.Copy, scale=taps[3][:])
            far.append(bank)

        energy = keep.tile([P, S], F32, name="energy")
        root_sb = keep.tile([P, S], F32, name="root_sb")
        gain = keep.tile([P, S], F32, name="gain")

        def inverse_root(cols, source):
            nc.scalar.activation(
                root_sb[:, cols], source, ACT.Abs_reciprocal_sqrt,
                scale=1.0 / 0.3, bias=0.5 / 0.3,
            )

        def gain_on_gpsimd(c):
            lo, hi = c * CHUNK, (c + 1) * CHUNK
            first = lo - 2 if c == 2 else lo
            nc.gpsimd.tensor_tensor(
                frames(PAIR, first, hi - first),
                frames(SQUARE, first, hi - first),
                frames(SQUARE, first, hi - first, 1),
                ALU.add,
            )
            nc.gpsimd.tensor_tensor(
                energy[:, lo:hi], frames(PAIR, lo, CHUNK), frames(PAIR, lo, CHUNK, 2), ALU.add
            )
            inverse_root(slice(lo, hi), energy[:, lo:hi])
            nc.scalar.activation(gain[:, lo:hi], root_sb[:, lo:hi], ACT.Square)

        def gain_by_transposes(c):
            lo, hi = c * CHUNK, (c + 1) * CHUNK
            energy_t = psum.tile([P, CHUNK], F32, name="energy_t", tag="turned%d" % c)
            for b in range(BLOCKS):
                for delay in range(4):
                    nc.tensor.matmul(
                        energy_t[:, b * P : (b + 1) * P],
                        frames(SQUARE, lo + b * P, P, delay),
                        identity[:],
                        start=(delay == 0),
                        stop=(delay == 3),
                        is_transpose=True,
                    )
            inverse_root(slice(lo, hi), energy_t[:])
            root = psum.tile([P, CHUNK], F32, name="root", tag="turned%d" % c)
            for b in range(BLOCKS):
                nc.tensor.transpose(
                    root[:, b * P : (b + 1) * P],
                    root_sb[:, lo + b * P : lo + (b + 1) * P],
                    identity[:],
                )
            nc.scalar.activation(gain[:, lo:hi], root[:], ACT.Square)

        gain_on_gpsimd(0)
        gain_by_transposes(1)
        gain_by_transposes(3)
        gain_on_gpsimd(2)

        echo = keep.tile([P, S], F32, name="echo")
        err = keep.tile([P, S], F32, name="err")
        result = keep.tile([P, S], F32, name="result")

        def tap_step(d, c):
            cols = slice(c * CHUNK, (c + 1) * CHUNK)
            nc.vector.scalar_tensor_tensor(
                frames(d, c * CHUNK, CHUNK) if d else echo[:, cols],
                far[c][:],
                taps[d][:],
                frames(d + 1, c * CHUNK, CHUNK, 1),
                ALU.mult,
                ALU.add,
            )

        def error(c):
            cols = slice(c * CHUNK, (c + 1) * CHUNK)
            nc.vector.tensor_tensor(err[:, cols], mic[c], echo[:, cols], ALU.subtract)

        def finish(c):
            cols = slice(c * CHUNK, (c + 1) * CHUNK)
            nc.vector.scalar_tensor_tensor(
                result[:, cols], gain[:, cols], 0.4, err[:, cols], ALU.add, ALU.mult
            )
            nc.sync.dma_start(out[:, cols], result[:, cols])

        tap_step(2, 0)
        tap_step(1, 0)
        tap_step(2, 1)
        tap_step(0, 0)
        tap_step(1, 1)
        error(0)
        tap_step(0, 1)
        tap_step(2, 2)
        error(1)
        tap_step(1, 2)
        tap_step(2, 3)
        tap_step(0, 2)
        tap_step(1, 3)
        error(2)
        tap_step(0, 3)
        finish(0)
        error(3)
        finish(1)
        finish(3)
        finish(2)
